import numpy as np
import ml_dtypes


def mxq(x, axis, fmt="e4m3"):
    dtype, down = {"e4m3": (ml_dtypes.float8_e4m3fn, 7), "e5m2": (ml_dtypes.float8_e5m2, 14)}[fmt]
    v = np.moveaxis(np.asarray(x, np.float32).astype(ml_dtypes.bfloat16).astype(np.float64), axis, -1)
    blocks = v.reshape(v.shape[:-1] + (-1, 32))
    amax = np.abs(blocks).max(-1, keepdims=True)
    byte = np.maximum(np.where(amax > 0, np.frexp(amax)[1] - 1 + 127, 0) - down, 1)
    scale = np.exp2(byte - 127.0)
    codes = (blocks / scale).astype(np.float32).astype(dtype).astype(np.float64)
    return np.moveaxis((codes * scale).reshape(v.shape), -1, axis)


WIDE = False


def mx_kscale(k):
    if not WIDE:
        return np.ones(k)
    levels = np.array([10, -10, 5, -5, 0])
    if k % 512:
        return np.exp2(np.random.permutation(np.resize(levels, k // 32))).repeat(32)
    a = np.empty((k // 512, 16))
    for p in range(k // 512):
        a[p, :8] = np.random.permutation(np.resize(levels, 8))
        for g in range(8):
            far = levels[np.abs(levels - a[p, g]) >= 10]
            a[p, g + 8] = far[np.random.randint(len(far))]
    return np.exp2(a.ravel()).repeat(32)


def f64(x):
    return np.asarray(x).astype(np.float64)


def striped(idx):
    return np.tile(idx.reshape(-1, 16).T, (8, 1)).astype(np.uint16)


def unstriped(offs):
    return offs[:16].T.reshape(-1).astype(np.int64)


def pack_weight(w):
    k, n = w.shape
    w = f64(np.asarray(w, np.float32).astype(ml_dtypes.bfloat16)).reshape(k // 32, 32, n)
    amax = np.abs(w).max(1)
    byte = np.clip(np.where(amax > 0, np.frexp(amax)[1] - 1 + 127 - 7, 1), 1, 254)
    scaled = (w * np.exp2(127.0 - byte)[:, None, :]).reshape(k, n).astype(np.float32)
    words = np.ascontiguousarray(scaled.reshape(k // 512, 128, 4, n).transpose(0, 1, 3, 2)).astype(ml_dtypes.float8_e4m3fn).view(np.uint8)
    return words, np.ascontiguousarray(byte.astype(np.uint8).reshape(k // 512, 16, n))


def unpack_weight(words, scales):
    g, p, n, _ = words.shape
    vals = np.ascontiguousarray(words).view(ml_dtypes.float8_e4m3fn).astype(np.float64) * np.repeat(np.exp2(scales.astype(np.float64) - 127.0), 8, axis=1)[..., None]
    return vals.transpose(0, 1, 3, 2).reshape(g * 512, n)

def planes(y):
    n, m = y.shape
    v = y.astype(np.float32).astype(ml_dtypes.bfloat16).astype(np.float64).reshape(n // 32, 32, m)
    top = np.abs(v).max(1)
    byte = np.clip(np.where(top > 0, np.frexp(top)[1] - 1 + 127 - 7, 1), 1, 254)
    codes = (v * np.exp2(127.0 - byte)[:, None, :]).reshape(n, m).astype(np.float32).astype(ml_dtypes.float8_e4m3fn).view(np.uint8)
    words = codes.reshape(n // 512, 128, 4, m).transpose(0, 1, 3, 2)
    return np.ascontiguousarray(words), np.ascontiguousarray(byte.astype(np.uint8).reshape(n // 512, 16, m))


K, T, S, V, N = 512, 1024, 512, 256, 512
P = 2 ** 7


def setup_inputs():
    n = np.random.standard_normal
    s = mx_kscale(K)[:, None]
    packed_xT = pack_weight(n((K, T)) * s)
    return {
        "x_words": packed_xT[0],
        "x_scales": packed_xT[1],
        "w1": (n((K, N)) / np.sqrt(K) / s).astype(np.float32),
        "frac": np.tile(np.random.uniform(0.05, 0.95, V), (P, 1)).astype(np.float32),
        "offs": striped(np.random.permutation(T)[:S]),
        "left": striped(np.random.permutation(S)[:V]),
        "right": striped(np.random.permutation(S)[:V]),
    }


def reference(x_words, x_scales, w1, frac, offs, left, right):
    xq = unpack_weight(x_words, x_scales)[:, unstriped(offs)]
    y = mxq(f64(w1), 0, "e4m3").T @ xq
    l = y[:, unstriped(left)]
    out_0 = l + (y[:, unstriped(right)] - l) * f64(frac)[:1]
    return (out_0,) + planes(out_0)

@@ -1,0 +1,153 @@
+import concourse.mybir as mybir
+
+K, T, S, V, N = 512, 1024, 512, 256, 512
+FLOPS = 2 * K * N * S
+
+F32 = mybir.dt.float32
+BF16 = mybir.dt.bfloat16
+I32 = mybir.dt.int32
+U32 = mybir.dt.uint32
+U16 = mybir.dt.uint16
+U8 = mybir.dt.uint8
+FP8X4 = mybir.dt.float8_e4m3fn_x4
+MULT = mybir.AluOpType.mult
+ADD = mybir.AluOpType.add
+
+P = 128
+PACK = 4
+
+
+def tile_picked_lerp_none_po_kernel(tc, x_words, x_scales, w1, frac, offs, left, right, out_0, out_1, out_2):
+    nc = tc.nc
+    with tc.tile_pool(name="held", bufs=1) as held, tc.psum_pool(name="psum", bufs=1) as psum:
+        offs_t = held.tile([P, S // 16], U16, name="offs_t")
+        left_t = held.tile([P, V // 16], U16, name="left_t")
+        right_t = held.tile([P, V // 16], U16, name="right_t")
+        xw = held.tile([P, T], I32, name="xw")
+        xs = held.tile([P, T], U8, name="xs")
+        xw_g = held.tile([P, S], U32, name="xw_g", align_bytes=64)
+        xs_g = held.tile([P, S], U8, name="xs_g", align_bytes=64)
+        fr = held.tile([P, V], F32, name="fr")
+        omf = held.tile([P, V], F32, name="omf")
+        w_raw = [held.tile([P, PACK, 256], F32, name=f"w_raw{h}") for h in range(2)]
+        w_bf = [[held.tile([P, 2, 64, PACK], BF16, name=f"w_bf{h}{u}", align_bytes=64) for u in range(2)] for h in range(2)]
+        wq = [held.tile([P, P], U32, name=f"wq{t}", align_bytes=64) for t in range(PACK)]
+        ws = [held.tile([P, P], U8, name=f"ws{t}", align_bytes=64) for t in range(PACK)]
+        y = [held.tile([P, S], F32, name=f"y{t}") for t in range(PACK)]
+
+        nc.vector.memset(xs[:].bitcast(I32), 0)
+        nc.sync.dma_start(offs_t[:], offs)
+        nc.sync.dma_start(xw[:], x_words[0].rearrange("p n r -> p (n r)").bitcast(I32))
+        for q in range(4):
+            nc.scalar.dma_start(xs[32 * q : 32 * q + 4, :].bitcast(I32), x_scales[0, 4 * q : 4 * q + 4, :].bitcast(I32))
+        w_rows = w1.rearrange("(p j) m -> p j m", j=PACK)
+        for h in range(2):
+            nc.sync.dma_start(w_raw[h][:], w_rows[:, :, 256 * h : 256 * h + 256])
+        nc.sync.dma_start(left_t[:], left)
+        nc.sync.dma_start(right_t[:], right)
+        nc.sync.dma_start(fr[:], frac)
+
+        nc.vector.tensor_copy(xw_g[:], xw[:].bitcast(U32).indirect(offs_t[:]))
+        nc.vector.tensor_copy(xs_g[:], xs[:].indirect(offs_t[:]))
+
+        def cast_w(copy, h, u):
+            src = w_raw[h][:].rearrange("p j (c t) -> p c t j", t=PACK)[:, :, 2 * u : 2 * u + 2, :]
+            copy(w_bf[h][u][:].rearrange("p t c j -> p c t j"), src)
+
+        def quant_w(h, t):
+            cols = slice(64 * h, 64 * h + 64)
+            nc.vector.quantize_mx(
+                out=wq[t][:, cols].bitcast(FP8X4),
+                scales=ws[t][:, cols],
+                in_=w_bf[h][t // 2][:, t % 2].rearrange("p c j -> p (c j)"),
+            )
+
+        def product(t, lo, hi):
+            bank = psum.tile([P, hi - lo], F32, name=f"bank{t}_{lo}")
+            nc.tensor.matmul_mx(
+                out=bank[:],
+                lhsT=wq[t][:].bitcast(FP8X4),
+                lhsT_scale=ws[t][:],
+                rhs=xw_g[:, lo:hi].bitcast(FP8X4),
+                rhs_scale=xs_g[:, lo:hi],
+                start=True,
+                stop=True,
+            )
+            nc.scalar.copy(y[t][:, lo:hi], bank[:])
+
+        cast_w(nc.scalar.copy, 0, 0)
+        cast_w(nc.scalar.copy, 0, 1)
+        cast_w(nc.vector.tensor_copy, 1, 0)
+        cast_w(nc.scalar.copy, 1, 1)
+        quant_w(0, 0)
+        quant_w(0, 1)
+        quant_w(1, 0)
+        product(0, 0, 256)
+        product(0, 256, 512)
+        quant_w(1, 1)
+        product(1, 0, 512)
+        for t in (2, 3):
+            quant_w(0, t)
+            quant_w(1, t)
+            product(t, 0, 512)
+        nc.vector.tensor_scalar(omf[:], fr[:], -1.0, 1.0, MULT, ADD)
+
+        out_rows = out_0.rearrange("(p t) v -> p t v", t=PACK)
+        pieces = [(0, 0, 256), (1, 0, 256), (2, 0, 256), (3, 0, 128), (3, 128, 256)]
+        la = [held.tile([P, hi - lo], F32, name=f"la{i}") for i, (t, lo, hi) in enumerate(pieces)]
+        rb = [held.tile([P, hi - lo], F32, name=f"rb{i}") for i, (t, lo, hi) in enumerate(pieces)]
+        o01 = held.tile([P, 2, V], F32, name="o01")
+        o23 = held.tile([P, 2, V], F32, name="o23")
+        o_pair = [o01, o23]
+        ob = [held.tile([P, 128, PACK], BF16, name=f"ob{h}", align_bytes=64) for h in range(2)]
+        ow = held.tile([P, V], U32, name="ow", align_bytes=64)
+        osc = held.tile([P, V], U8, name="osc", align_bytes=64)
+        words_out = out_1[0].rearrange("p n r -> p (n r)").bitcast(I32)
+
+        def g_left(i):
+            t, lo, hi = pieces[i]
+            nc.vector.tensor_tensor(la[i][:], y[t][:].indirect(left_t[:, lo // 16 : hi // 16]), omf[:, lo:hi], MULT)
+
+        def g_right(i):
+            t, lo, hi = pieces[i]
+            nc.vector.tensor_tensor(rb[i][:], y[t][:].indirect(right_t[:, lo // 16 : hi // 16]), fr[:, lo:hi], MULT)
+
+        def add(i):
+            t, lo, hi = pieces[i]
+            dst = o_pair[t // 2][:, t % 2, lo:hi]
+            nc.vector.tensor_tensor(dst, la[i][:], rb[i][:], ADD)
+            nc.sync.dma_start(out_rows[:, t, lo:hi], dst)
+
+        def cast_o(copy, h, u):
+            src = o_pair[u][:, :, 128 * h : 128 * h + 128].rearrange("p t v -> p v t")
+            copy(ob[h][:, :, 2 * u : 2 * u + 2], src)
+
+        def quant_o(h):
+            cols = slice(128 * h, 128 * h + 128)
+            nc.vector.quantize_mx(out=ow[:, cols].bitcast(FP8X4), scales=osc[:, cols], in_=ob[h][:].rearrange("p v t -> p (v t)"))
+            nc.sync.dma_start(words_out[:, cols], ow[:, cols].bitcast(I32))
+
+        g_right(0)
+        g_left(0)
+        g_right(1)
+        add(0)
+        g_left(1)
+        g_right(2)
+        add(1)
+        cast_o(nc.scalar.copy, 0, 0)
+        cast_o(nc.scalar.copy, 1, 0)
+        g_left(2)
+        g_right(3)
+        add(2)
+        g_left(3)
+        g_right(4)
+        add(3)
+        g_left(4)
+        cast_o(nc.vector.tensor_copy, 0, 1)
+        add(4)
+        quant_o(0)
+        cast_o(nc.vector.tensor_copy, 1, 1)
+        quant_o(1)
+        for q in range(4):
+            eng = nc.scalar if q % 2 == 0 else nc.sync
+            eng.dma_start(out_2[0, 4 * q : 4 * q + 4, :].bitcast(I32), osc[32 * q : 32 * q + 4, :].bitcast(I32))

@@ -1,4 +1,5 @@
 import concourse.mybir as mybir
+from concourse.masks import make_identity
 
 K, T, S, V, N = 512, 1024, 512, 256, 512
 FLOPS = 2 * K * N * S
@@ -30,124 +31,132 @@ def tile_picked_lerp_none_po_kernel(tc, x_words, x_scales, w1, frac, offs, left,
         fr = held.tile([P, V], F32, name="fr")
         omf = held.tile([P, V], F32, name="omf")
         w_raw = [held.tile([P, PACK, 256], F32, name=f"w_raw{h}") for h in range(2)]
-        w_bf = [[held.tile([P, 2, 64, PACK], BF16, name=f"w_bf{h}{u}", align_bytes=64) for u in range(2)] for h in range(2)]
-        wq = [held.tile([P, P], U32, name=f"wq{t}", align_bytes=64) for t in range(PACK)]
-        ws = [held.tile([P, P], U8, name=f"ws{t}", align_bytes=64) for t in range(PACK)]
+        w_bf = [held.tile([P, 2, P, PACK], BF16, name=f"w_bf{u}", align_bytes=64) for u in range(2)]
+        wq = held.tile([P, PACK * P], U32, name="wq", align_bytes=64)
+        ws = held.tile([P, PACK * P], U8, name="ws", align_bytes=64)
         y = [held.tile([P, S], F32, name=f"y{t}") for t in range(PACK)]
 
         nc.vector.memset(xs[:].bitcast(I32), 0)
         nc.sync.dma_start(offs_t[:], offs)
-        nc.sync.dma_start(xw[:], x_words[0].rearrange("p n r -> p (n r)").bitcast(I32))
-        for q in range(4):
-            nc.scalar.dma_start(xs[32 * q : 32 * q + 4, :].bitcast(I32), x_scales[0, 4 * q : 4 * q + 4, :].bitcast(I32))
         w_rows = w1.rearrange("(p j) m -> p j m", j=PACK)
+        x_rows = x_words[0].rearrange("p n r -> p (n r)").bitcast(I32)
+        nc.sync.dma_start(xw[:, 0 : T // 2], x_rows[:, 0 : T // 2])
+        for q in range(4):
+            nc.sync.dma_start(xs[32 * q : 32 * q + 4, :].bitcast(I32), x_scales[0, 4 * q : 4 * q + 4, :].bitcast(I32))
+        nc.sync.dma_start(xw[:, T // 2 : T], x_rows[:, T // 2 : T])
         for h in range(2):
             nc.sync.dma_start(w_raw[h][:], w_rows[:, :, 256 * h : 256 * h + 256])
+        nc.sync.dma_start(fr[:], frac)
         nc.sync.dma_start(left_t[:], left)
         nc.sync.dma_start(right_t[:], right)
-        nc.sync.dma_start(fr[:], frac)
+        ident = held.tile([P, P], F32, name="ident")
+        make_identity(nc, ident[:])
 
-        nc.vector.tensor_copy(xw_g[:], xw[:].bitcast(U32).indirect(offs_t[:]))
         nc.vector.tensor_copy(xs_g[:], xs[:].indirect(offs_t[:]))
 
-        def cast_w(copy, h, u):
-            src = w_raw[h][:].rearrange("p j (c t) -> p c t j", t=PACK)[:, :, 2 * u : 2 * u + 2, :]
-            copy(w_bf[h][u][:].rearrange("p t c j -> p c t j"), src)
+        nc.vector.tensor_copy(xw_g[:], xw[:].bitcast(U32).indirect(offs_t[:]))
 
-        def quant_w(h, t):
-            cols = slice(64 * h, 64 * h + 64)
+        def cast_w(copy, h, t0, t1):
+            src = w_raw[h][:].rearrange("p j (c t) -> p c t j", t=PACK)[:, :, t0:t1, :]
+            copy(w_bf[t0 // 2][:, t0 % 2 : t0 % 2 + t1 - t0, 64 * h : 64 * h + 64, :].rearrange("p t c j -> p c t j"), src)
+
+        def quant_w(t0, t1):
+            cols = slice(P * t0, P * t1)
             nc.vector.quantize_mx(
-                out=wq[t][:, cols].bitcast(FP8X4),
-                scales=ws[t][:, cols],
-                in_=w_bf[h][t // 2][:, t % 2].rearrange("p c j -> p (c j)"),
+                out=wq[:, cols].bitcast(FP8X4),
+                scales=ws[:, cols],
+                in_=w_bf[t0 // 2][:, t0 % 2 : t0 % 2 + t1 - t0].rearrange("p t c j -> p (t c j)"),
             )
 
-        def product(t, lo, hi):
-            bank = psum.tile([P, hi - lo], F32, name=f"bank{t}_{lo}")
+        def product(t, lo, hi, copy):
+            bank = psum.tile([P, hi - lo], F32, name=f"bank{t}_{lo}", tag=f"bank{t}_{lo}")
             nc.tensor.matmul_mx(
                 out=bank[:],
-                lhsT=wq[t][:].bitcast(FP8X4),
-                lhsT_scale=ws[t][:],
+                lhsT=wq[:, P * t : P * t + P].bitcast(FP8X4),
+                lhsT_scale=ws[:, P * t : P * t + P],
                 rhs=xw_g[:, lo:hi].bitcast(FP8X4),
                 rhs_scale=xs_g[:, lo:hi],
                 start=True,
                 stop=True,
             )
-            nc.scalar.copy(y[t][:, lo:hi], bank[:])
+            copy(y[t][:, lo:hi], bank[:])
 
-        cast_w(nc.scalar.copy, 0, 0)
-        cast_w(nc.scalar.copy, 0, 1)
-        cast_w(nc.vector.tensor_copy, 1, 0)
-        cast_w(nc.scalar.copy, 1, 1)
-        quant_w(0, 0)
+        cast_w(nc.scalar.copy, 0, 0, 2)
+        cast_w(nc.vector.tensor_copy, 0, 2, 4)
+        cast_w(nc.vector.tensor_copy, 1, 0, 2)
+        cast_w(nc.scalar.copy, 1, 2, 4)
         quant_w(0, 1)
-        quant_w(1, 0)
-        product(0, 0, 256)
-        product(0, 256, 512)
-        quant_w(1, 1)
-        product(1, 0, 512)
-        for t in (2, 3):
-            quant_w(0, t)
-            quant_w(1, t)
-            product(t, 0, 512)
+        product(0, 0, 256, nc.scalar.copy)
+        product(0, 256, 512, nc.scalar.copy)
+        quant_w(1, 2)
+        quant_w(2, 4)
         nc.vector.tensor_scalar(omf[:], fr[:], -1.0, 1.0, MULT, ADD)
+        for t in (1, 2, 3):
+            product(t, 0, 512, nc.scalar.copy)
 
-        out_rows = out_0.rearrange("(p t) v -> p t v", t=PACK)
         pieces = [(0, 0, 256), (1, 0, 256), (2, 0, 256), (3, 0, 128), (3, 128, 256)]
-        la = [held.tile([P, hi - lo], F32, name=f"la{i}") for i, (t, lo, hi) in enumerate(pieces)]
-        rb = [held.tile([P, hi - lo], F32, name=f"rb{i}") for i, (t, lo, hi) in enumerate(pieces)]
-        o01 = held.tile([P, 2, V], F32, name="o01")
-        o23 = held.tile([P, 2, V], F32, name="o23")
-        o_pair = [o01, o23]
-        ob = [held.tile([P, 128, PACK], BF16, name=f"ob{h}", align_bytes=64) for h in range(2)]
+        la = held.tile([P, PACK * V], F32, name="la")
+        rb = held.tile([P, PACK * V], F32, name="rb")
+        o = held.tile([P, PACK * V], F32, name="o")
+        ob = held.tile([P, V, PACK], BF16, name="ob", align_bytes=64)
         ow = held.tile([P, V], U32, name="ow", align_bytes=64)
         osc = held.tile([P, V], U8, name="osc", align_bytes=64)
         words_out = out_1[0].rearrange("p n r -> p (n r)").bitcast(I32)
 
         def g_left(i):
             t, lo, hi = pieces[i]
-            nc.vector.tensor_tensor(la[i][:], y[t][:].indirect(left_t[:, lo // 16 : hi // 16]), omf[:, lo:hi], MULT)
+            nc.vector.tensor_tensor(la[:, t * V + lo : t * V + hi], y[t][:].indirect(left_t[:, lo // 16 : hi // 16]), omf[:, lo:hi], MULT)
 
         def g_right(i):
             t, lo, hi = pieces[i]
-            nc.vector.tensor_tensor(rb[i][:], y[t][:].indirect(right_t[:, lo // 16 : hi // 16]), fr[:, lo:hi], MULT)
+            nc.vector.tensor_tensor(rb[:, t * V + lo : t * V + hi], y[t][:].indirect(right_t[:, lo // 16 : hi // 16]), fr[:, lo:hi], MULT)
 
-        def add(i):
-            t, lo, hi = pieces[i]
-            dst = o_pair[t // 2][:, t % 2, lo:hi]
-            nc.vector.tensor_tensor(dst, la[i][:], rb[i][:], ADD)
-            nc.sync.dma_start(out_rows[:, t, lo:hi], dst)
+        out_flat = out_0.rearrange("(p t) v -> p (t v)", t=PACK)
 
-        def cast_o(copy, h, u):
-            src = o_pair[u][:, :, 128 * h : 128 * h + 128].rearrange("p t v -> p v t")
-            copy(ob[h][:, :, 2 * u : 2 * u + 2], src)
+        def add(lo, hi):
+            nc.vector.tensor_tensor(o[:, lo:hi], la[:, lo:hi], rb[:, lo:hi], ADD)
+            nc.sync.dma_start(out_flat[:, lo:hi], o[:, lo:hi])
+
+        bank_back = psum.tile([P, 2 * V], F32, name="bank_back")
+
+        def add_on_tensor(t):
+            turned = held.tile([P, 2, P], F32, name=f"turned{t}")
+            bank_sum = psum.tile([P, 2, P], F32, name=f"bank_sum{t}", tag=f"bank{t + 2}_0")
+            for h in range(2):
+                cols = slice(V * t + P * h, V * t + P * h + P)
+                nc.tensor.matmul(bank_sum[:, h, :], rb[:, cols], ident[:], start=True, stop=False, is_transpose=True)
+                nc.tensor.matmul(bank_sum[:, h, :], la[:, cols], ident[:], start=False, stop=True, is_transpose=True)
+            nc.scalar.copy(turned[:], bank_sum[:])
+            for h in range(2):
+                nc.tensor.transpose(bank_back[:, V * t + P * h : V * t + P * h + P], turned[:, h, :], ident[:])
+
+        def cast_o(copy, h):
+            cols = slice(128 * h, 128 * h + 128)
+            copy(ob[:, cols, :], o[:].rearrange("p (t v) -> p v t", t=PACK)[:, cols, :])
 
         def quant_o(h):
             cols = slice(128 * h, 128 * h + 128)
-            nc.vector.quantize_mx(out=ow[:, cols].bitcast(FP8X4), scales=osc[:, cols], in_=ob[h][:].rearrange("p v t -> p (v t)"))
-            nc.sync.dma_start(words_out[:, cols], ow[:, cols].bitcast(I32))
+            nc.vector.quantize_mx(out=ow[:, cols].bitcast(FP8X4), scales=osc[:, cols], in_=ob[:, cols, :].rearrange("p v t -> p (v t)"))
 
-        g_right(0)
-        g_left(0)
-        g_right(1)
-        add(0)
-        g_left(1)
+        for t in range(2):
+            g_right(t)
+            g_left(t)
+            add_on_tensor(t)
+        nc.scalar.copy(o[:, 0 : 2 * V], bank_back[:])
+        nc.scalar.dma_start(out_flat[:, 0 : 2 * V], o[:, 0 : 2 * V])
         g_right(2)
-        add(1)
-        cast_o(nc.scalar.copy, 0, 0)
-        cast_o(nc.scalar.copy, 1, 0)
         g_left(2)
         g_right(3)
-        add(2)
         g_left(3)
         g_right(4)
-        add(3)
+        add(512, 896)
+        cast_o(nc.scalar.copy, 0)
         g_left(4)
-        cast_o(nc.vector.tensor_copy, 0, 1)
-        add(4)
+        add(896, 1024)
+        cast_o(nc.vector.tensor_copy, 1)
         quant_o(0)
-        cast_o(nc.vector.tensor_copy, 1, 1)
         quant_o(1)
+        nc.sync.dma_start(words_out, ow[:].bitcast(I32))
         for q in range(4):
             eng = nc.scalar if q % 2 == 0 else nc.sync
             eng.dma_start(out_2[0, 4 * q : 4 * q + 4, :].bitcast(I32), osc[32 * q : 32 * q + 4, :].bitcast(I32))

@@ -31,7 +31,8 @@ def tile_picked_lerp_none_po_kernel(tc, x_words, x_scales, w1, frac, offs, left,
         fr = held.tile([P, V], F32, name="fr")
         omf = held.tile([P, V], F32, name="omf")
         w_raw = [held.tile([P, PACK, 256], F32, name=f"w_raw{h}") for h in range(2)]
-        w_bf = [held.tile([P, 2, P, PACK], BF16, name=f"w_bf{u}", align_bytes=64) for u in range(2)]
+        w_lo = [held.tile([P, 2, 64, PACK], BF16, name=f"w_lo{h}", align_bytes=64) for h in range(2)]
+        w_hi = held.tile([P, 2, P, PACK], BF16, name="w_hi", align_bytes=64)
         wq = held.tile([P, PACK * P], U32, name="wq", align_bytes=64)
         ws = held.tile([P, PACK * P], U8, name="ws", align_bytes=64)
         y = [held.tile([P, S], F32, name=f"y{t}") for t in range(PACK)]
@@ -39,14 +40,13 @@ def tile_picked_lerp_none_po_kernel(tc, x_words, x_scales, w1, frac, offs, left,
         nc.vector.memset(xs[:].bitcast(I32), 0)
         nc.sync.dma_start(offs_t[:], offs)
         w_rows = w1.rearrange("(p j) m -> p j m", j=PACK)
-        x_rows = x_words[0].rearrange("p n r -> p (n r)").bitcast(I32)
-        nc.sync.dma_start(xw[:, 0 : T // 2], x_rows[:, 0 : T // 2])
-        for q in range(4):
-            nc.sync.dma_start(xs[32 * q : 32 * q + 4, :].bitcast(I32), x_scales[0, 4 * q : 4 * q + 4, :].bitcast(I32))
-        nc.sync.dma_start(xw[:, T // 2 : T], x_rows[:, T // 2 : T])
-        for h in range(2):
-            nc.sync.dma_start(w_raw[h][:], w_rows[:, :, 256 * h : 256 * h + 256])
+        nc.sync.dma_start(w_raw[0][:, 0:2, :], w_rows[:, 0:2, 0:256])
+        for r in range(4):
+            nc.sync.dma_start(xs[r:P:32, :].bitcast(I32), x_scales[0, r:16:4, :].bitcast(I32))
+        nc.sync.dma_start(w_raw[0][:, 2:4, :], w_rows[:, 2:4, 0:256])
+        nc.sync.dma_start(xw[:], x_words[0].rearrange("p n r -> p (n r)").bitcast(I32))
         nc.sync.dma_start(fr[:], frac)
+        nc.sync.dma_start(w_raw[1][:], w_rows[:, :, 256:512])
         nc.sync.dma_start(left_t[:], left)
         nc.sync.dma_start(right_t[:], right)
         ident = held.tile([P, P], F32, name="ident")
@@ -54,19 +54,13 @@ def tile_picked_lerp_none_po_kernel(tc, x_words, x_scales, w1, frac, offs, left,
 
         nc.vector.tensor_copy(xs_g[:], xs[:].indirect(offs_t[:]))
 
-        nc.vector.tensor_copy(xw_g[:], xw[:].bitcast(U32).indirect(offs_t[:]))
+        def cast_w(copy, h, u, j0=0, j1=PACK):
+            src = w_raw[h][:].rearrange("p j (c t) -> p c t j", t=PACK)[:, :, 2 * u : 2 * u + 2, j0:j1]
+            dst = w_lo[h][:] if u == 0 else w_hi[:, :, 64 * h : 64 * h + 64, :]
+            copy(dst.rearrange("p t c j -> p c t j")[:, :, :, j0:j1], src)
 
-        def cast_w(copy, h, t0, t1):
-            src = w_raw[h][:].rearrange("p j (c t) -> p c t j", t=PACK)[:, :, t0:t1, :]
-            copy(w_bf[t0 // 2][:, t0 % 2 : t0 % 2 + t1 - t0, 64 * h : 64 * h + 64, :].rearrange("p t c j -> p c t j"), src)
-
-        def quant_w(t0, t1):
-            cols = slice(P * t0, P * t1)
-            nc.vector.quantize_mx(
-                out=wq[:, cols].bitcast(FP8X4),
-                scales=ws[:, cols],
-                in_=w_bf[t0 // 2][:, t0 % 2 : t0 % 2 + t1 - t0].rearrange("p t c j -> p (t c j)"),
-            )
+        def quant_w(src, lo, hi):
+            nc.vector.quantize_mx(out=wq[:, lo:hi].bitcast(FP8X4), scales=ws[:, lo:hi], in_=src[:].rearrange("p t c j -> p (t c j)"))
 
         def product(t, lo, hi, copy):
             bank = psum.tile([P, hi - lo], F32, name=f"bank{t}_{lo}", tag=f"bank{t}_{lo}")
@@ -81,17 +75,21 @@ def tile_picked_lerp_none_po_kernel(tc, x_words, x_scales, w1, frac, offs, left,
             )
             copy(y[t][:, lo:hi], bank[:])
 
-        cast_w(nc.scalar.copy, 0, 0, 2)
-        cast_w(nc.vector.tensor_copy, 0, 2, 4)
-        cast_w(nc.vector.tensor_copy, 1, 0, 2)
-        cast_w(nc.scalar.copy, 1, 2, 4)
-        quant_w(0, 1)
-        product(0, 0, 256, nc.scalar.copy)
-        product(0, 256, 512, nc.scalar.copy)
-        quant_w(1, 2)
-        quant_w(2, 4)
-        nc.vector.tensor_scalar(omf[:], fr[:], -1.0, 1.0, MULT, ADD)
-        for t in (1, 2, 3):
+        cast_w(nc.scalar.copy, 0, 0, 0, 2)
+        cast_w(nc.scalar.copy, 0, 0, 2, 4)
+        cast_w(nc.scalar.copy, 0, 1)
+        nc.scalar.activation(omf[:], fr[:], mybir.ActivationFunctionType.Copy, bias=1.0, scale=-1.0)
+        quant_w(w_lo[0], 0, P)
+        for lo, hi in ((0, 256), (256, 384), (384, 512)):
+            nc.vector.tensor_copy(xw_g[:, lo:hi], xw[:].bitcast(U32).indirect(offs_t[:, lo // 16 : hi // 16]))
+            product(0, lo, hi, nc.scalar.copy)
+        cast_w(nc.vector.tensor_copy, 1, 0)
+        cast_w(nc.vector.tensor_copy, 1, 1)
+        quant_w(w_lo[1], P, 2 * P)
+        quant_w(w_hi, 2 * P, 4 * P)
+        product(1, 0, 256, nc.scalar.copy)
+        product(1, 256, 512, nc.scalar.copy)
+        for t in (2, 3):
             product(t, 0, 512, nc.scalar.copy)
 
         pieces = [(0, 0, 256), (1, 0, 256), (2, 0, 256), (3, 0, 128), (3, 128, 256)]
@@ -117,18 +115,18 @@ def tile_picked_lerp_none_po_kernel(tc, x_words, x_scales, w1, frac, offs, left,
             nc.vector.tensor_tensor(o[:, lo:hi], la[:, lo:hi], rb[:, lo:hi], ADD)
             nc.sync.dma_start(out_flat[:, lo:hi], o[:, lo:hi])
 
-        bank_back = psum.tile([P, 2 * V], F32, name="bank_back")
+        turned = held.tile([P, 2, 2, P], F32, name="turned")
 
-        def add_on_tensor(t):
-            turned = held.tile([P, 2, P], F32, name=f"turned{t}")
-            bank_sum = psum.tile([P, 2, P], F32, name=f"bank_sum{t}", tag=f"bank{t + 2}_0")
-            for h in range(2):
-                cols = slice(V * t + P * h, V * t + P * h + P)
-                nc.tensor.matmul(bank_sum[:, h, :], rb[:, cols], ident[:], start=True, stop=False, is_transpose=True)
-                nc.tensor.matmul(bank_sum[:, h, :], la[:, cols], ident[:], start=False, stop=True, is_transpose=True)
-            nc.scalar.copy(turned[:], bank_sum[:])
-            for h in range(2):
-                nc.tensor.transpose(bank_back[:, V * t + P * h : V * t + P * h + P], turned[:, h, :], ident[:])
+        def sum_turned(bank, i, h):
+            cols = slice(V * i + P * h, V * i + P * h + P)
+            nc.tensor.matmul(bank, rb[:, cols], ident[:], start=True, stop=False, is_transpose=True)
+            nc.tensor.matmul(bank, la[:, cols], ident[:], start=False, stop=True, is_transpose=True)
+
+        def turn_back(h):
+            bank = psum.tile([P, 2, P], F32, name=f"bank_back{h}", tag=f"bank0_{256 * h}")
+            for t in range(2):
+                nc.tensor.transpose(bank[:, t, :], turned[:, h, t, :], ident[:])
+            nc.scalar.copy(o[:].rearrange("p (t v) -> p t v", t=PACK)[:, 0:2, P * h : P * h + P], bank[:])
 
         def cast_o(copy, h):
             cols = slice(128 * h, 128 * h + 128)
@@ -138,11 +136,20 @@ def tile_picked_lerp_none_po_kernel(tc, x_words, x_scales, w1, frac, offs, left,
             cols = slice(128 * h, 128 * h + 128)
             nc.vector.quantize_mx(out=ow[:, cols].bitcast(FP8X4), scales=osc[:, cols], in_=ob[:, cols, :].rearrange("p v t -> p (v t)"))
 
-        for t in range(2):
-            g_right(t)
-            g_left(t)
-            add_on_tensor(t)
-        nc.scalar.copy(o[:, 0 : 2 * V], bank_back[:])
+        g_right(0)
+        g_left(0)
+        sum0 = psum.tile([P, 2, P], F32, name="sum0", tag="bank2_0")
+        for h in range(2):
+            sum_turned(sum0[:, h, :], 0, h)
+        nc.scalar.copy(turned[:, :, :, 0:64], sum0[:].rearrange("p h (t c) -> p h t c", t=2))
+        g_right(1)
+        g_left(1)
+        for h in range(2):
+            sum1 = psum.tile([P, P], F32, name=f"sum1{h}", tag=f"bank{3 - h}_0")
+            sum_turned(sum1[:], 1, h)
+            nc.scalar.copy(turned[:, h, :, 64:P], sum1[:].rearrange("p (t c) -> p t c", t=2))
+        for h in range(2):
+            turn_back(h)
         nc.scalar.dma_start(out_flat[:, 0 : 2 * V], o[:, 0 : 2 * V])
         g_right(2)
         g_left(2)
@@ -157,6 +164,6 @@ def tile_picked_lerp_none_po_kernel(tc, x_words, x_scales, w1, frac, offs, left,
         quant_o(0)
         quant_o(1)
         nc.sync.dma_start(words_out, ow[:].bitcast(I32))
-        for q in range(4):
-            eng = nc.scalar if q % 2 == 0 else nc.sync
-            eng.dma_start(out_2[0, 4 * q : 4 * q + 4, :].bitcast(I32), osc[32 * q : 32 * q + 4, :].bitcast(I32))
+        for r in range(4):
+            eng = nc.scalar if r % 2 == 0 else nc.sync
+            eng.dma_start(out_2[0, r:16:4, :].bitcast(I32), osc[r:P:32, :].bitcast(I32))

@@ -50,7 +50,8 @@ def tile_picked_lerp_none_po_kernel(tc, x_words, x_scales, w1, frac, offs, left,
         nc.sync.dma_start(left_t[:], left)
         nc.sync.dma_start(right_t[:], right)
         ident = held.tile([P, P], F32, name="ident")
-        make_identity(nc, ident[:])
+        nc.vector.memset(ident[:], 0.0)
+        make_identity(nc, ident[:], nomemset=True)
 
         nc.vector.tensor_copy(xs_g[:], xs[:].indirect(offs_t[:]))
 

@@ -112,9 +112,11 @@ def tile_picked_lerp_none_po_kernel(tc, x_words, x_scales, w1, frac, offs, left,
 
         out_flat = out_0.rearrange("(p t) v -> p (t v)", t=PACK)
 
+        def upper(ap, h):
+            return ap.rearrange("p (t v) -> p t v", t=PACK)[:, 2:4, P * h : P * h + P]
+
         def add(lo, hi):
             nc.vector.tensor_tensor(o[:, lo:hi], la[:, lo:hi], rb[:, lo:hi], ADD)
-            nc.sync.dma_start(out_flat[:, lo:hi], o[:, lo:hi])
 
         turned = held.tile([P, 2, 2, P], F32, name="turned")
 
@@ -139,28 +141,33 @@ def tile_picked_lerp_none_po_kernel(tc, x_words, x_scales, w1, frac, offs, left,
 
         g_right(0)
         g_left(0)
-        sum0 = psum.tile([P, 2, P], F32, name="sum0", tag="bank2_0")
+        sum0 = psum.tile([P, 2, P], F32, name="sum0", tag="sum0")
         for h in range(2):
             sum_turned(sum0[:, h, :], 0, h)
         nc.scalar.copy(turned[:, :, :, 0:64], sum0[:].rearrange("p h (t c) -> p h t c", t=2))
         g_right(1)
+        sum1 = [psum.tile([P, P], F32, name=f"sum1{h}", tag=("bank0_384", "bank1_0")[h]) for h in range(2)]
+        for h in range(2):
+            nc.tensor.matmul(sum1[h][:], rb[:, V + P * h : V + P * h + P], ident[:], start=True, stop=False, is_transpose=True)
         g_left(1)
         for h in range(2):
-            sum1 = psum.tile([P, P], F32, name=f"sum1{h}", tag=f"bank{3 - h}_0")
-            sum_turned(sum1[:], 1, h)
-            nc.scalar.copy(turned[:, h, :, 64:P], sum1[:].rearrange("p (t c) -> p t c", t=2))
+            nc.tensor.matmul(sum1[h][:], la[:, V + P * h : V + P * h + P], ident[:], start=False, stop=True, is_transpose=True)
+            nc.scalar.copy(turned[:, h, :, 64:P], sum1[h][:].rearrange("p (t c) -> p t c", t=2))
         for h in range(2):
             turn_back(h)
-        nc.scalar.dma_start(out_flat[:, 0 : 2 * V], o[:, 0 : 2 * V])
+        nc.sync.dma_start(out_flat[:, 0 : 2 * V], o[:, 0 : 2 * V])
         g_right(2)
         g_left(2)
         g_right(3)
         g_left(3)
         g_right(4)
-        add(512, 896)
+        nc.vector.tensor_tensor(upper(o[:], 0), upper(la[:], 0), upper(rb[:], 0), ADD)
+        nc.sync.dma_start(upper(out_flat, 0), upper(o[:], 0))
         cast_o(nc.scalar.copy, 0)
         g_left(4)
+        add(640, 768)
         add(896, 1024)
+        nc.sync.dma_start(upper(out_flat, 1), upper(o[:], 1))
         cast_o(nc.vector.tensor_copy, 1)
         quant_o(0)
         quant_o(1)

@@ -56,9 +56,9 @@ def tile_picked_lerp_none_po_kernel(tc, x_words, x_scales, w1, frac, offs, left,
         nc.vector.tensor_copy(xs_g[:], xs[:].indirect(offs_t[:]))
 
         def cast_w(copy, h, u, j0=0, j1=PACK):
-            src = w_raw[h][:].rearrange("p j (c t) -> p c t j", t=PACK)[:, :, 2 * u : 2 * u + 2, j0:j1]
+            src = w_raw[h][:].rearrange("p j (c t) -> p c j t", t=PACK)[:, :, j0:j1, 2 * u : 2 * u + 2]
             dst = w_lo[h][:] if u == 0 else w_hi[:, :, 64 * h : 64 * h + 64, :]
-            copy(dst.rearrange("p t c j -> p c t j")[:, :, :, j0:j1], src)
+            copy(dst.rearrange("p t c j -> p c j t")[:, :, j0:j1, :], src)
 
         def quant_w(src, lo, hi):
             nc.vector.quantize_mx(out=wq[:, lo:hi].bitcast(FP8X4), scales=ws[:, lo:hi], in_=src[:].rearrange("p t c j -> p (t c j)"))
@@ -133,7 +133,8 @@ def tile_picked_lerp_none_po_kernel(tc, x_words, x_scales, w1, frac, offs, left,
 
         def cast_o(copy, h):
             cols = slice(128 * h, 128 * h + 128)
-            copy(ob[:, cols, :], o[:].rearrange("p (t v) -> p v t", t=PACK)[:, cols, :])
+            src = o[:].rearrange("p (t v) -> p t v", t=PACK)[:, :, cols]
+            copy(ob[:, cols, :].rearrange("p (c i) t -> p c t i", i=4), src.rearrange("p t (c i) -> p c t i", i=4))
 
         def quant_o(h):
             cols = slice(128 * h, 128 * h + 128)

@@ -25,10 +25,9 @@ def tile_picked_lerp_none_po_kernel(tc, x_words, x_scales, w1, frac, offs, left,
         left_t = held.tile([P, V // 16], U16, name="left_t")
         right_t = held.tile([P, V // 16], U16, name="right_t")
         xw = held.tile([P, T], I32, name="xw")
-        xs = held.tile([P, T], U8, name="xs")
+        xs = held.tile([P, T], U8, name="xs", tag="xs")
         xw_g = held.tile([P, S], U32, name="xw_g", align_bytes=64)
         xs_g = held.tile([P, S], U8, name="xs_g", align_bytes=64)
-        fr = held.tile([P, V], F32, name="fr")
         omf = held.tile([P, V], F32, name="omf")
         w_raw = [held.tile([P, PACK, 256], F32, name=f"w_raw{h}") for h in range(2)]
         w_lo = [held.tile([P, 2, 64, PACK], BF16, name=f"w_lo{h}", align_bytes=64) for h in range(2)]
@@ -45,15 +44,16 @@ def tile_picked_lerp_none_po_kernel(tc, x_words, x_scales, w1, frac, offs, left,
             nc.sync.dma_start(xs[r:P:32, :].bitcast(I32), x_scales[0, r:16:4, :].bitcast(I32))
         nc.sync.dma_start(w_raw[0][:, 2:4, :], w_rows[:, 2:4, 0:256])
         nc.sync.dma_start(xw[:], x_words[0].rearrange("p n r -> p (n r)").bitcast(I32))
-        nc.sync.dma_start(fr[:], frac)
-        nc.sync.dma_start(w_raw[1][:], w_rows[:, :, 256:512])
         nc.sync.dma_start(left_t[:], left)
         nc.sync.dma_start(right_t[:], right)
+        nc.sync.dma_start(w_raw[1][:], w_rows[:, :, 256:512])
         ident = held.tile([P, P], F32, name="ident")
         nc.vector.memset(ident[:], 0.0)
         make_identity(nc, ident[:], nomemset=True)
 
         nc.vector.tensor_copy(xs_g[:], xs[:].indirect(offs_t[:]))
+        fr = held.tile([P, V], F32, name="fr", tag="xs")
+        nc.sync.dma_start(fr[:], frac)
 
         def cast_w(copy, h, u, j0=0, j1=PACK):
             src = w_raw[h][:].rearrange("p j (c t) -> p c j t", t=PACK)[:, :, j0:j1, 2 * u : 2 * u + 2]
@@ -79,11 +79,11 @@ def tile_picked_lerp_none_po_kernel(tc, x_words, x_scales, w1, frac, offs, left,
         cast_w(nc.scalar.copy, 0, 0, 0, 2)
         cast_w(nc.scalar.copy, 0, 0, 2, 4)
         cast_w(nc.scalar.copy, 0, 1)
-        nc.scalar.activation(omf[:], fr[:], mybir.ActivationFunctionType.Copy, bias=1.0, scale=-1.0)
         quant_w(w_lo[0], 0, P)
         for lo, hi in ((0, 256), (256, 384), (384, 512)):
             nc.vector.tensor_copy(xw_g[:, lo:hi], xw[:].bitcast(U32).indirect(offs_t[:, lo // 16 : hi // 16]))
             product(0, lo, hi, nc.scalar.copy)
+        nc.scalar.activation(omf[:], fr[:], mybir.ActivationFunctionType.Copy, bias=1.0, scale=-1.0)
         cast_w(nc.vector.tensor_copy, 1, 0)
         cast_w(nc.vector.tensor_copy, 1, 1)
         quant_w(w_lo[1], P, 2 * P)
@@ -93,7 +93,6 @@ def tile_picked_lerp_none_po_kernel(tc, x_words, x_scales, w1, frac, offs, left,
         for t in (2, 3):
             product(t, 0, 512, nc.scalar.copy)
 
-        pieces = [(0, 0, 256), (1, 0, 256), (2, 0, 256), (3, 0, 128), (3, 128, 256)]
         la = held.tile([P, PACK * V], F32, name="la")
         rb = held.tile([P, PACK * V], F32, name="rb")
         o = held.tile([P, PACK * V], F32, name="o")
@@ -102,18 +101,13 @@ def tile_picked_lerp_none_po_kernel(tc, x_words, x_scales, w1, frac, offs, left,
         osc = held.tile([P, V], U8, name="osc", align_bytes=64)
         words_out = out_1[0].rearrange("p n r -> p (n r)").bitcast(I32)
 
-        def g_left(i):
-            t, lo, hi = pieces[i]
-            nc.vector.tensor_tensor(la[:, t * V + lo : t * V + hi], y[t][:].indirect(left_t[:, lo // 16 : hi // 16]), omf[:, lo:hi], MULT)
+        def g_left(t):
+            nc.vector.tensor_tensor(la[:, t * V : t * V + V], y[t][:].indirect(left_t[:]), omf[:], MULT)
 
-        def g_right(i):
-            t, lo, hi = pieces[i]
-            nc.vector.tensor_tensor(rb[:, t * V + lo : t * V + hi], y[t][:].indirect(right_t[:, lo // 16 : hi // 16]), fr[:, lo:hi], MULT)
+        def g_right(t):
+            nc.vector.tensor_tensor(rb[:, t * V : t * V + V], y[t][:].indirect(right_t[:]), fr[:], MULT)
 
         out_flat = out_0.rearrange("(p t) v -> p (t v)", t=PACK)
-
-        def upper(ap, h):
-            return ap.rearrange("p (t v) -> p t v", t=PACK)[:, 2:4, P * h : P * h + P]
 
         def add(lo, hi):
             nc.vector.tensor_tensor(o[:, lo:hi], la[:, lo:hi], rb[:, lo:hi], ADD)
@@ -131,8 +125,8 @@ def tile_picked_lerp_none_po_kernel(tc, x_words, x_scales, w1, frac, offs, left,
                 nc.tensor.transpose(bank[:, t, :], turned[:, h, t, :], ident[:])
             nc.scalar.copy(o[:].rearrange("p (t v) -> p t v", t=PACK)[:, 0:2, P * h : P * h + P], bank[:])
 
-        def cast_o(copy, h):
-            cols = slice(128 * h, 128 * h + 128)
+        def cast_o(copy, lo, hi):
+            cols = slice(lo, hi)
             src = o[:].rearrange("p (t v) -> p t v", t=PACK)[:, :, cols]
             copy(ob[:, cols, :].rearrange("p (c i) t -> p c t i", i=4), src.rearrange("p t (c i) -> p c t i", i=4))
 
@@ -158,18 +152,17 @@ def tile_picked_lerp_none_po_kernel(tc, x_words, x_scales, w1, frac, offs, left,
             turn_back(h)
         nc.sync.dma_start(out_flat[:, 0 : 2 * V], o[:, 0 : 2 * V])
         g_right(2)
-        g_left(2)
         g_right(3)
+        g_left(2)
         g_left(3)
-        g_right(4)
-        nc.vector.tensor_tensor(upper(o[:], 0), upper(la[:], 0), upper(rb[:], 0), ADD)
-        nc.sync.dma_start(upper(out_flat, 0), upper(o[:], 0))
-        cast_o(nc.scalar.copy, 0)
-        g_left(4)
-        add(640, 768)
+        add(512, 768)
+        add(768, 896)
+        nc.sync.dma_start(out_flat[:, 512:896], o[:, 512:896])
+        cast_o(nc.scalar.copy, 0, 64)
         add(896, 1024)
-        nc.sync.dma_start(upper(out_flat, 1), upper(o[:], 1))
-        cast_o(nc.vector.tensor_copy, 1)
+        nc.sync.dma_start(out_flat[:, 896:1024], o[:, 896:1024])
+        cast_o(nc.vector.tensor_copy, 64, 128)
+        cast_o(nc.vector.tensor_copy, 128, 256)
         quant_o(0)
         quant_o(1)
         nc.sync.dma_start(words_out, ow[:].bitcast(I32))

@@ -90,8 +90,6 @@ def tile_picked_lerp_none_po_kernel(tc, x_words, x_scales, w1, frac, offs, left,
         quant_w(w_hi, 2 * P, 4 * P)
         product(1, 0, 256, nc.scalar.copy)
         product(1, 256, 512, nc.scalar.copy)
-        for t in (2, 3):
-            product(t, 0, 512, nc.scalar.copy)
 
         la = held.tile([P, PACK * V], F32, name="la")
         rb = held.tile([P, PACK * V], F32, name="rb")
@@ -106,6 +104,14 @@ def tile_picked_lerp_none_po_kernel(tc, x_words, x_scales, w1, frac, offs, left,
 
         def g_right(t):
             nc.vector.tensor_tensor(rb[:, t * V : t * V + V], y[t][:].indirect(right_t[:]), fr[:], MULT)
+
+        lv = held.tile([P, 2 * V], F32, name="lv")
+
+        def s_left(t):
+            nc.scalar.activation(lv[:, (t - 2) * V : (t - 1) * V], y[t][:].indirect(left_t[:]), mybir.ActivationFunctionType.Copy)
+
+        def weigh(t):
+            nc.vector.tensor_tensor(la[:, t * V : t * V + V], lv[:, (t - 2) * V : (t - 1) * V], omf[:], MULT)
 
         out_flat = out_0.rearrange("(p t) v -> p (t v)", t=PACK)
 
@@ -134,12 +140,15 @@ def tile_picked_lerp_none_po_kernel(tc, x_words, x_scales, w1, frac, offs, left,
             cols = slice(128 * h, 128 * h + 128)
             nc.vector.quantize_mx(out=ow[:, cols].bitcast(FP8X4), scales=osc[:, cols], in_=ob[:, cols, :].rearrange("p v t -> p (v t)"))
 
+        product(2, 0, 512, nc.scalar.copy)
+        product(3, 0, 512, nc.scalar.copy)
         g_right(0)
         g_left(0)
         sum0 = psum.tile([P, 2, P], F32, name="sum0", tag="sum0")
         for h in range(2):
             sum_turned(sum0[:, h, :], 0, h)
         nc.scalar.copy(turned[:, :, :, 0:64], sum0[:].rearrange("p h (t c) -> p h t c", t=2))
+        s_left(2)
         g_right(1)
         sum1 = [psum.tile([P, P], F32, name=f"sum1{h}", tag=("bank0_384", "bank1_0")[h]) for h in range(2)]
         for h in range(2):
@@ -148,13 +157,14 @@ def tile_picked_lerp_none_po_kernel(tc, x_words, x_scales, w1, frac, offs, left,
         for h in range(2):
             nc.tensor.matmul(sum1[h][:], la[:, V + P * h : V + P * h + P], ident[:], start=False, stop=True, is_transpose=True)
             nc.scalar.copy(turned[:, h, :, 64:P], sum1[h][:].rearrange("p (t c) -> p t c", t=2))
+        s_left(3)
         for h in range(2):
             turn_back(h)
         nc.sync.dma_start(out_flat[:, 0 : 2 * V], o[:, 0 : 2 * V])
         g_right(2)
         g_right(3)
-        g_left(2)
-        g_left(3)
+        weigh(2)
+        weigh(3)
         add(512, 768)
         add(768, 896)
         nc.sync.dma_start(out_flat[:, 512:896], o[:, 512:896])

@@ -31,7 +31,7 @@ def tile_picked_lerp_none_po_kernel(tc, x_words, x_scales, w1, frac, offs, left,
         omf = held.tile([P, V], F32, name="omf")
         w_raw = [held.tile([P, PACK, 256], F32, name=f"w_raw{h}") for h in range(2)]
         w_lo = [held.tile([P, 2, 64, PACK], BF16, name=f"w_lo{h}", align_bytes=64) for h in range(2)]
-        w_hi = held.tile([P, 2, P, PACK], BF16, name="w_hi", align_bytes=64)
+        w_hi = held.tile([P, 2, P, PACK], BF16, name="w_hi", tag="w_hi", align_bytes=64)
         wq = held.tile([P, PACK * P], U32, name="wq", align_bytes=64)
         ws = held.tile([P, PACK * P], U8, name="ws", align_bytes=64)
         y = [held.tile([P, S], F32, name=f"y{t}") for t in range(PACK)]
@@ -63,8 +63,8 @@ def tile_picked_lerp_none_po_kernel(tc, x_words, x_scales, w1, frac, offs, left,
         def quant_w(src, lo, hi):
             nc.vector.quantize_mx(out=wq[:, lo:hi].bitcast(FP8X4), scales=ws[:, lo:hi], in_=src[:].rearrange("p t c j -> p (t c j)"))
 
-        def product(t, lo, hi, copy):
-            bank = psum.tile([P, hi - lo], F32, name=f"bank{t}_{lo}", tag=f"bank{t}_{lo}")
+        def product(t, lo, hi, copy, tag=None):
+            bank = psum.tile([P, hi - lo], F32, name=f"bank{t}_{lo}", tag=tag or f"bank{t}_{lo}")
             nc.tensor.matmul_mx(
                 out=bank[:],
                 lhsT=wq[:, P * t : P * t + P].bitcast(FP8X4),
@@ -91,8 +91,9 @@ def tile_picked_lerp_none_po_kernel(tc, x_words, x_scales, w1, frac, offs, left,
         product(1, 0, 256, nc.scalar.copy)
         product(1, 256, 512, nc.scalar.copy)
 
-        la = held.tile([P, PACK * V], F32, name="la")
-        rb = held.tile([P, PACK * V], F32, name="rb")
+        weighed = held.tile([P, 2, PACK * V], F32, name="weighed", tag="w_hi", align_bytes=64)
+        la = weighed[:, 0, :]
+        rb = weighed[:, 1, :]
         o = held.tile([P, PACK * V], F32, name="o")
         ob = held.tile([P, V, PACK], BF16, name="ob", align_bytes=64)
         ow = held.tile([P, V], U32, name="ow", align_bytes=64)
@@ -107,11 +108,11 @@ def tile_picked_lerp_none_po_kernel(tc, x_words, x_scales, w1, frac, offs, left,
 
         lv = held.tile([P, 2 * V], F32, name="lv")
 
-        def s_left(t):
-            nc.scalar.activation(lv[:, (t - 2) * V : (t - 1) * V], y[t][:].indirect(left_t[:]), mybir.ActivationFunctionType.Copy)
+        def s_left(t, n):
+            nc.scalar.activation(lv[:, (t - 2) * V : (t - 2) * V + n], y[t][:].indirect(left_t[:, 0 : n // 16]), mybir.ActivationFunctionType.Copy)
 
-        def weigh(t):
-            nc.vector.tensor_tensor(la[:, t * V : t * V + V], lv[:, (t - 2) * V : (t - 1) * V], omf[:], MULT)
+        def weigh(t, n):
+            nc.vector.tensor_tensor(la[:, t * V : t * V + n], lv[:, (t - 2) * V : (t - 2) * V + n], omf[:, 0:n], MULT)
 
         out_flat = out_0.rearrange("(p t) v -> p (t v)", t=PACK)
 
@@ -140,15 +141,17 @@ def tile_picked_lerp_none_po_kernel(tc, x_words, x_scales, w1, frac, offs, left,
             cols = slice(128 * h, 128 * h + 128)
             nc.vector.quantize_mx(out=ow[:, cols].bitcast(FP8X4), scales=osc[:, cols], in_=ob[:, cols, :].rearrange("p v t -> p (v t)"))
 
-        product(2, 0, 512, nc.scalar.copy)
-        product(3, 0, 512, nc.scalar.copy)
+        product(2, 0, 256, nc.scalar.copy)
+        product(2, 256, 512, nc.scalar.copy, "bank0_0")
+        product(3, 0, 256, nc.scalar.copy)
+        product(3, 256, 512, nc.scalar.copy, "bank0_256")
         g_right(0)
         g_left(0)
         sum0 = psum.tile([P, 2, P], F32, name="sum0", tag="sum0")
         for h in range(2):
             sum_turned(sum0[:, h, :], 0, h)
         nc.scalar.copy(turned[:, :, :, 0:64], sum0[:].rearrange("p h (t c) -> p h t c", t=2))
-        s_left(2)
+        s_left(2, V)
         g_right(1)
         sum1 = [psum.tile([P, P], F32, name=f"sum1{h}", tag=("bank0_384", "bank1_0")[h]) for h in range(2)]
         for h in range(2):
@@ -157,22 +160,23 @@ def tile_picked_lerp_none_po_kernel(tc, x_words, x_scales, w1, frac, offs, left,
         for h in range(2):
             nc.tensor.matmul(sum1[h][:], la[:, V + P * h : V + P * h + P], ident[:], start=False, stop=True, is_transpose=True)
             nc.scalar.copy(turned[:, h, :, 64:P], sum1[h][:].rearrange("p (t c) -> p t c", t=2))
-        s_left(3)
+        s_left(3, P)
         for h in range(2):
             turn_back(h)
         nc.sync.dma_start(out_flat[:, 0 : 2 * V], o[:, 0 : 2 * V])
         g_right(2)
         g_right(3)
-        weigh(2)
-        weigh(3)
+        nc.vector.tensor_tensor(la[:, 3 * V + P : 4 * V], y[3][:].indirect(left_t[:, P // 16 : V // 16]), omf[:, P:V], MULT)
+        weigh(2, V)
+        weigh(3, P)
         add(512, 768)
         add(768, 896)
         nc.sync.dma_start(out_flat[:, 512:896], o[:, 512:896])
-        cast_o(nc.scalar.copy, 0, 64)
         add(896, 1024)
         nc.sync.dma_start(out_flat[:, 896:1024], o[:, 896:1024])
-        cast_o(nc.vector.tensor_copy, 64, 128)
-        cast_o(nc.vector.tensor_copy, 128, 256)
+        cast_o(nc.scalar.copy, 160, 256)
+        cast_o(nc.vector.tensor_copy, 0, 128)
+        cast_o(nc.vector.tensor_copy, 128, 160)
         quant_o(0)
         quant_o(1)
         nc.sync.dma_start(words_out, ow[:].bitcast(I32))

@@ -30,8 +30,8 @@ def tile_picked_lerp_none_po_kernel(tc, x_words, x_scales, w1, frac, offs, left,
         xs_g = held.tile([P, S], U8, name="xs_g", align_bytes=64)
         omf = held.tile([P, V], F32, name="omf")
         w_raw = [held.tile([P, PACK, 256], F32, name=f"w_raw{h}") for h in range(2)]
-        w_lo = [held.tile([P, 2, 64, PACK], BF16, name=f"w_lo{h}", align_bytes=64) for h in range(2)]
-        w_hi = held.tile([P, 2, P, PACK], BF16, name="w_hi", tag="w_hi", align_bytes=64)
+        w_lo = [held.tile([P, 2, 64, PACK], BF16, name=f"w_lo{h}", tag=f"w_lo{h}", align_bytes=64) for h in range(2)]
+        w_hi = held.tile([P, 2, P, PACK], BF16, name="w_hi", align_bytes=64)
         wq = held.tile([P, PACK * P], U32, name="wq", align_bytes=64)
         ws = held.tile([P, PACK * P], U8, name="ws", align_bytes=64)
         y = [held.tile([P, S], F32, name=f"y{t}") for t in range(PACK)]
@@ -91,7 +91,7 @@ def tile_picked_lerp_none_po_kernel(tc, x_words, x_scales, w1, frac, offs, left,
         product(1, 0, 256, nc.scalar.copy)
         product(1, 256, 512, nc.scalar.copy)
 
-        weighed = held.tile([P, 2, PACK * V], F32, name="weighed", tag="w_hi", align_bytes=64)
+        weighed = held.tile([P, 2, PACK * V], F32, name="weighed", tag="w_lo1", align_bytes=64)
         la = weighed[:, 0, :]
         rb = weighed[:, 1, :]
         o = held.tile([P, PACK * V], F32, name="o")
@@ -108,11 +108,11 @@ def tile_picked_lerp_none_po_kernel(tc, x_words, x_scales, w1, frac, offs, left,
 
         lv = held.tile([P, 2 * V], F32, name="lv")
 
-        def s_left(t, n):
-            nc.scalar.activation(lv[:, (t - 2) * V : (t - 2) * V + n], y[t][:].indirect(left_t[:, 0 : n // 16]), mybir.ActivationFunctionType.Copy)
+        def s_left(t, lo):
+            nc.scalar.activation(lv[:, (t - 2) * V + lo : (t - 1) * V], y[t][:].indirect(left_t[:, lo // 16 : V // 16]), mybir.ActivationFunctionType.Copy)
 
-        def weigh(t, n):
-            nc.vector.tensor_tensor(la[:, t * V : t * V + n], lv[:, (t - 2) * V : (t - 2) * V + n], omf[:, 0:n], MULT)
+        def weigh(t, lo):
+            nc.vector.tensor_tensor(la[:, t * V + lo : t * V + V], lv[:, (t - 2) * V + lo : (t - 1) * V], omf[:, lo:V], MULT)
 
         out_flat = out_0.rearrange("(p t) v -> p (t v)", t=PACK)
 
@@ -151,7 +151,7 @@ def tile_picked_lerp_none_po_kernel(tc, x_words, x_scales, w1, frac, offs, left,
         for h in range(2):
             sum_turned(sum0[:, h, :], 0, h)
         nc.scalar.copy(turned[:, :, :, 0:64], sum0[:].rearrange("p h (t c) -> p h t c", t=2))
-        s_left(2, V)
+        s_left(2, 0)
         g_right(1)
         sum1 = [psum.tile([P, P], F32, name=f"sum1{h}", tag=("bank0_384", "bank1_0")[h]) for h in range(2)]
         for h in range(2):
@@ -166,17 +166,17 @@ def tile_picked_lerp_none_po_kernel(tc, x_words, x_scales, w1, frac, offs, left,
         nc.sync.dma_start(out_flat[:, 0 : 2 * V], o[:, 0 : 2 * V])
         g_right(2)
         g_right(3)
-        nc.vector.tensor_tensor(la[:, 3 * V + P : 4 * V], y[3][:].indirect(left_t[:, P // 16 : V // 16]), omf[:, P:V], MULT)
-        weigh(2, V)
+        nc.vector.tensor_tensor(la[:, 3 * V : 3 * V + P], y[3][:].indirect(left_t[:, 0 : P // 16]), omf[:, 0:P], MULT)
+        weigh(2, 0)
         weigh(3, P)
         add(512, 768)
         add(768, 896)
         nc.sync.dma_start(out_flat[:, 512:896], o[:, 512:896])
         add(896, 1024)
         nc.sync.dma_start(out_flat[:, 896:1024], o[:, 896:1024])
-        cast_o(nc.scalar.copy, 160, 256)
+        cast_o(nc.scalar.copy, 192, 256)
         cast_o(nc.vector.tensor_copy, 0, 128)
-        cast_o(nc.vector.tensor_copy, 128, 160)
+        cast_o(nc.vector.tensor_copy, 128, 192)
         quant_o(0)
         quant_o(1)
         nc.sync.dma_start(words_out, ow[:].bitcast(I32))

@@ -34,7 +34,7 @@ def tile_picked_lerp_none_po_kernel(tc, x_words, x_scales, w1, frac, offs, left,
         w_hi = held.tile([P, 2, P, PACK], BF16, name="w_hi", align_bytes=64)
         wq = held.tile([P, PACK * P], U32, name="wq", align_bytes=64)
         ws = held.tile([P, PACK * P], U8, name="ws", align_bytes=64)
-        y = [held.tile([P, S], F32, name=f"y{t}") for t in range(PACK)]
+        y = [held.tile([P, S], F32, name=f"y{t}", tag=f"y{t}") for t in range(PACK)]
 
         nc.vector.memset(xs[:].bitcast(I32), 0)
         nc.sync.dma_start(offs_t[:], offs)
@@ -94,7 +94,6 @@ def tile_picked_lerp_none_po_kernel(tc, x_words, x_scales, w1, frac, offs, left,
         weighed = held.tile([P, 2, PACK * V], F32, name="weighed", tag="w_lo1", align_bytes=64)
         la = weighed[:, 0, :]
         rb = weighed[:, 1, :]
-        o = held.tile([P, PACK * V], F32, name="o")
         ob = held.tile([P, V, PACK], BF16, name="ob", align_bytes=64)
         ow = held.tile([P, V], U32, name="ow", align_bytes=64)
         osc = held.tile([P, V], U8, name="osc", align_bytes=64)
@@ -108,11 +107,11 @@ def tile_picked_lerp_none_po_kernel(tc, x_words, x_scales, w1, frac, offs, left,
 
         lv = held.tile([P, 2 * V], F32, name="lv")
 
-        def s_left(t, lo):
-            nc.scalar.activation(lv[:, (t - 2) * V + lo : (t - 1) * V], y[t][:].indirect(left_t[:, lo // 16 : V // 16]), mybir.ActivationFunctionType.Copy)
+        def s_left(t, lo, hi):
+            nc.scalar.activation(lv[:, (t - 2) * V + lo : (t - 2) * V + hi], y[t][:].indirect(left_t[:, lo // 16 : hi // 16]), mybir.ActivationFunctionType.Copy)
 
-        def weigh(t, lo):
-            nc.vector.tensor_tensor(la[:, t * V + lo : t * V + V], lv[:, (t - 2) * V + lo : (t - 1) * V], omf[:, lo:V], MULT)
+        def weigh(t, lo, hi):
+            nc.vector.tensor_tensor(la[:, t * V + lo : t * V + hi], lv[:, (t - 2) * V + lo : (t - 2) * V + hi], omf[:, lo:hi], MULT)
 
         out_flat = out_0.rearrange("(p t) v -> p (t v)", t=PACK)
 
@@ -145,13 +144,14 @@ def tile_picked_lerp_none_po_kernel(tc, x_words, x_scales, w1, frac, offs, left,
         product(2, 256, 512, nc.scalar.copy, "bank0_0")
         product(3, 0, 256, nc.scalar.copy)
         product(3, 256, 512, nc.scalar.copy, "bank0_256")
+        s_left(2, 0, V)
         g_right(0)
         g_left(0)
         sum0 = psum.tile([P, 2, P], F32, name="sum0", tag="sum0")
         for h in range(2):
             sum_turned(sum0[:, h, :], 0, h)
         nc.scalar.copy(turned[:, :, :, 0:64], sum0[:].rearrange("p h (t c) -> p h t c", t=2))
-        s_left(2, 0)
+        s_left(3, P, V)
         g_right(1)
         sum1 = [psum.tile([P, P], F32, name=f"sum1{h}", tag=("bank0_384", "bank1_0")[h]) for h in range(2)]
         for h in range(2):
@@ -160,25 +160,26 @@ def tile_picked_lerp_none_po_kernel(tc, x_words, x_scales, w1, frac, offs, left,
         for h in range(2):
             nc.tensor.matmul(sum1[h][:], la[:, V + P * h : V + P * h + P], ident[:], start=False, stop=True, is_transpose=True)
             nc.scalar.copy(turned[:, h, :, 64:P], sum1[h][:].rearrange("p (t c) -> p t c", t=2))
-        s_left(3, P)
+        s_left(3, 0, P)
+        g_right(2)
+        g_right(3)
+        o = held.tile([P, PACK * V], F32, name="o", tag="y3")
         for h in range(2):
             turn_back(h)
         nc.sync.dma_start(out_flat[:, 0 : 2 * V], o[:, 0 : 2 * V])
-        g_right(2)
-        g_right(3)
-        nc.vector.tensor_tensor(la[:, 3 * V : 3 * V + P], y[3][:].indirect(left_t[:, 0 : P // 16]), omf[:, 0:P], MULT)
-        weigh(2, 0)
-        weigh(3, P)
+        weigh(2, 0, V)
+        weigh(3, P, V)
+        weigh(3, 0, P)
         add(512, 768)
-        add(768, 896)
-        nc.sync.dma_start(out_flat[:, 512:896], o[:, 512:896])
+        nc.sync.dma_start(out_flat[:, 512:768], o[:, 512:768])
         add(896, 1024)
-        nc.sync.dma_start(out_flat[:, 896:1024], o[:, 896:1024])
+        add(768, 896)
+        nc.sync.dma_start(out_flat[:, 768:1024], o[:, 768:1024])
         cast_o(nc.scalar.copy, 192, 256)
-        cast_o(nc.vector.tensor_copy, 0, 128)
         cast_o(nc.vector.tensor_copy, 128, 192)
-        quant_o(0)
+        cast_o(nc.vector.tensor_copy, 0, 128)
         quant_o(1)
+        quant_o(0)
         nc.sync.dma_start(words_out, ow[:].bitcast(I32))
         for r in range(4):
             eng = nc.scalar if r % 2 == 0 else nc.sync

@@ -37,9 +37,9 @@ def tile_picked_lerp_none_po_kernel(tc, x_words, x_scales, w1, frac, offs, left,
         y = [held.tile([P, S], F32, name=f"y{t}", tag=f"y{t}") for t in range(PACK)]
 
         nc.vector.memset(xs[:].bitcast(I32), 0)
-        nc.sync.dma_start(offs_t[:], offs)
         w_rows = w1.rearrange("(p j) m -> p j m", j=PACK)
         nc.sync.dma_start(w_raw[0][:, 0:2, :], w_rows[:, 0:2, 0:256])
+        nc.sync.dma_start(offs_t[:], offs)
         for r in range(4):
             nc.sync.dma_start(xs[r:P:32, :].bitcast(I32), x_scales[0, r:16:4, :].bitcast(I32))
         nc.sync.dma_start(w_raw[0][:, 2:4, :], w_rows[:, 2:4, 0:256])
@@ -154,17 +154,17 @@ def tile_picked_lerp_none_po_kernel(tc, x_words, x_scales, w1, frac, offs, left,
         s_left(3, P, V)
         g_right(1)
         sum1 = [psum.tile([P, P], F32, name=f"sum1{h}", tag=("bank0_384", "bank1_0")[h]) for h in range(2)]
-        for h in range(2):
+        for h in (1, 0):
             nc.tensor.matmul(sum1[h][:], rb[:, V + P * h : V + P * h + P], ident[:], start=True, stop=False, is_transpose=True)
         g_left(1)
-        for h in range(2):
+        for h in (1, 0):
             nc.tensor.matmul(sum1[h][:], la[:, V + P * h : V + P * h + P], ident[:], start=False, stop=True, is_transpose=True)
             nc.scalar.copy(turned[:, h, :, 64:P], sum1[h][:].rearrange("p (t c) -> p t c", t=2))
         s_left(3, 0, P)
         g_right(2)
         g_right(3)
         o = held.tile([P, PACK * V], F32, name="o", tag="y3")
-        for h in range(2):
+        for h in (1, 0):
             turn_back(h)
         nc.sync.dma_start(out_flat[:, 0 : 2 * V], o[:, 0 : 2 * V])
         weigh(2, 0, V)
@@ -175,9 +175,9 @@ def tile_picked_lerp_none_po_kernel(tc, x_words, x_scales, w1, frac, offs, left,
         add(896, 1024)
         add(768, 896)
         nc.sync.dma_start(out_flat[:, 768:1024], o[:, 768:1024])
-        cast_o(nc.scalar.copy, 192, 256)
-        cast_o(nc.vector.tensor_copy, 128, 192)
-        cast_o(nc.vector.tensor_copy, 0, 128)
+        cast_o(nc.vector.tensor_copy, 128, 256)
+        cast_o(nc.scalar.copy, 0, 80)
+        cast_o(nc.vector.tensor_copy, 80, 128)
         quant_o(1)
         quant_o(0)
         nc.sync.dma_start(words_out, ow[:].bitcast(I32))

@@ -41,7 +41,7 @@ def tile_picked_lerp_none_po_kernel(tc, x_words, x_scales, w1, frac, offs, left,
         nc.sync.dma_start(w_raw[0][:, 0:2, :], w_rows[:, 0:2, 0:256])
         nc.sync.dma_start(offs_t[:], offs)
         for r in range(4):
-            nc.sync.dma_start(xs[r:P:32, :].bitcast(I32), x_scales[0, r:16:4, :].bitcast(I32))
+            (nc.sync if r % 2 == 0 else nc.scalar).dma_start(xs[r:P:32, :].bitcast(I32), x_scales[0, r:16:4, :].bitcast(I32))
         nc.sync.dma_start(w_raw[0][:, 2:4, :], w_rows[:, 2:4, 0:256])
         nc.sync.dma_start(xw[:], x_words[0].rearrange("p n r -> p (n r)").bitcast(I32))
         nc.sync.dma_start(left_t[:], left)

@@ -30,7 +30,7 @@ def tile_picked_lerp_none_po_kernel(tc, x_words, x_scales, w1, frac, offs, left,
         xs_g = held.tile([P, S], U8, name="xs_g", align_bytes=64)
         omf = held.tile([P, V], F32, name="omf")
         w_raw = [held.tile([P, PACK, 256], F32, name=f"w_raw{h}") for h in range(2)]
-        w_lo = [held.tile([P, 2, 64, PACK], BF16, name=f"w_lo{h}", tag=f"w_lo{h}", align_bytes=64) for h in range(2)]
+        w_lo = [held.tile([P, 64, 2, PACK], BF16, name=f"w_lo{h}", tag=f"w_lo{h}", align_bytes=64) for h in range(2)]
         w_hi = held.tile([P, 2, P, PACK], BF16, name="w_hi", align_bytes=64)
         wq = held.tile([P, PACK * P], U32, name="wq", align_bytes=64)
         ws = held.tile([P, PACK * P], U8, name="ws", align_bytes=64)
@@ -57,8 +57,11 @@ def tile_picked_lerp_none_po_kernel(tc, x_words, x_scales, w1, frac, offs, left,
 
         def cast_w(copy, h, u, j0=0, j1=PACK):
             src = w_raw[h][:].rearrange("p j (c t) -> p c j t", t=PACK)[:, :, j0:j1, 2 * u : 2 * u + 2]
-            dst = w_lo[h][:] if u == 0 else w_hi[:, :, 64 * h : 64 * h + 64, :]
-            copy(dst.rearrange("p t c j -> p c j t")[:, :, j0:j1, :], src)
+            if u == 0:
+                dst = w_lo[h][:].rearrange("p c t j -> p c j t")
+            else:
+                dst = w_hi[:, :, 64 * h : 64 * h + 64, :].rearrange("p t c j -> p c j t")
+            copy(dst[:, :, j0:j1, :], src)
 
         def quant_w(src, lo, hi):
             nc.vector.quantize_mx(out=wq[:, lo:hi].bitcast(FP8X4), scales=ws[:, lo:hi], in_=src[:].rearrange("p t c j -> p (t c j)"))
@@ -134,7 +137,7 @@ def tile_picked_lerp_none_po_kernel(tc, x_words, x_scales, w1, frac, offs, left,
         def cast_o(copy, lo, hi):
             cols = slice(lo, hi)
             src = o[:].rearrange("p (t v) -> p t v", t=PACK)[:, :, cols]
-            copy(ob[:, cols, :].rearrange("p (c i) t -> p c t i", i=4), src.rearrange("p t (c i) -> p c t i", i=4))
+            copy(ob[:, cols, :].rearrange("p (c i) t -> p c t i", i=2), src.rearrange("p t (c i) -> p c t i", i=2))
 
         def quant_o(h):
             cols = slice(128 * h, 128 * h + 128)
@@ -150,7 +153,7 @@ def tile_picked_lerp_none_po_kernel(tc, x_words, x_scales, w1, frac, offs, left,
         sum0 = psum.tile([P, 2, P], F32, name="sum0", tag="sum0")
         for h in range(2):
             sum_turned(sum0[:, h, :], 0, h)
-        nc.scalar.copy(turned[:, :, :, 0:64], sum0[:].rearrange("p h (t c) -> p h t c", t=2))
+        nc.scalar.copy(turned[:, :, :, 0:64], sum0[:].rearrange("p h (c t) -> p h t c", t=2))
         s_left(3, P, V)
         g_right(1)
         sum1 = [psum.tile([P, P], F32, name=f"sum1{h}", tag=("bank0_384", "bank1_0")[h]) for h in range(2)]
@@ -159,7 +162,7 @@ def tile_picked_lerp_none_po_kernel(tc, x_words, x_scales, w1, frac, offs, left,
         g_left(1)
         for h in (1, 0):
             nc.tensor.matmul(sum1[h][:], la[:, V + P * h : V + P * h + P], ident[:], start=False, stop=True, is_transpose=True)
-            nc.scalar.copy(turned[:, h, :, 64:P], sum1[h][:].rearrange("p (t c) -> p t c", t=2))
+            nc.scalar.copy(turned[:, h, :, 64:P], sum1[h][:].rearrange("p (c t) -> p t c", t=2))
         s_left(3, 0, P)
         g_right(2)
         g_right(3)

import concourse.mybir as mybir
from concourse.masks import make_identity

K, T, S, V, N = 512, 1024, 512, 256, 512
FLOPS = 2 * K * N * S

F32 = mybir.dt.float32
BF16 = mybir.dt.bfloat16
I32 = mybir.dt.int32
U32 = mybir.dt.uint32
U16 = mybir.dt.uint16
U8 = mybir.dt.uint8
FP8X4 = mybir.dt.float8_e4m3fn_x4
MULT = mybir.AluOpType.mult
ADD = mybir.AluOpType.add

P = 128
PACK = 4


def tile_picked_lerp_none_po_kernel(tc, x_words, x_scales, w1, frac, offs, left, right, out_0, out_1, out_2):
    nc = tc.nc
    with tc.tile_pool(name="held", bufs=1) as held, tc.psum_pool(name="psum", bufs=1) as psum:
        offs_t = held.tile([P, S // 16], U16, name="offs_t")
        left_t = held.tile([P, V // 16], U16, name="left_t")
        right_t = held.tile([P, V // 16], U16, name="right_t")
        xw = held.tile([P, T], I32, name="xw")
        xs = held.tile([P, T], U8, name="xs", tag="xs")
        xw_g = held.tile([P, S], U32, name="xw_g", align_bytes=64)
        xs_g = held.tile([P, S], U8, name="xs_g", align_bytes=64)
        omf = held.tile([P, V], F32, name="omf")
        w_raw = [held.tile([P, PACK, 256], F32, name=f"w_raw{h}") for h in range(2)]
        w_lo = [held.tile([P, 64, 2, PACK], BF16, name=f"w_lo{h}", tag=f"w_lo{h}", align_bytes=64) for h in range(2)]
        w_hi = held.tile([P, 2, P, PACK], BF16, name="w_hi", align_bytes=64)
        wq = held.tile([P, PACK * P], U32, name="wq", align_bytes=64)
        ws = held.tile([P, PACK * P], U8, name="ws", align_bytes=64)
        y = [held.tile([P, S], F32, name=f"y{t}", tag=f"y{t}") for t in range(PACK)]

        nc.vector.memset(xs[:].bitcast(I32), 0)
        w_rows = w1.rearrange("(p j) m -> p j m", j=PACK)
        nc.sync.dma_start(w_raw[0][:, 0:2, :], w_rows[:, 0:2, 0:256])
        nc.sync.dma_start(offs_t[:], offs)
        for r in range(4):
            (nc.sync if r % 2 == 0 else nc.scalar).dma_start(xs[r:P:32, :].bitcast(I32), x_scales[0, r:16:4, :].bitcast(I32))
        nc.sync.dma_start(w_raw[0][:, 2:4, :], w_rows[:, 2:4, 0:256])
        nc.sync.dma_start(xw[:], x_words[0].rearrange("p n r -> p (n r)").bitcast(I32))
        nc.sync.dma_start(left_t[:], left)
        nc.sync.dma_start(right_t[:], right)
        nc.sync.dma_start(w_raw[1][:], w_rows[:, :, 256:512])
        ident = held.tile([P, P], F32, name="ident")
        nc.vector.memset(ident[:], 0.0)
        make_identity(nc, ident[:], nomemset=True)

        nc.vector.tensor_copy(xs_g[:], xs[:].indirect(offs_t[:]))
        fr = held.tile([P, V], F32, name="fr", tag="xs")
        nc.sync.dma_start(fr[:], frac)

        def cast_w(copy, h, u, j0=0, j1=PACK):
            src = w_raw[h][:].rearrange("p j (c t) -> p c j t", t=PACK)[:, :, j0:j1, 2 * u : 2 * u + 2]
            if u == 0:
                dst = w_lo[h][:].rearrange("p c t j -> p c j t")
            else:
                dst = w_hi[:, :, 64 * h : 64 * h + 64, :].rearrange("p t c j -> p c j t")
            copy(dst[:, :, j0:j1, :], src)

        def quant_w(src, lo, hi):
            nc.vector.quantize_mx(out=wq[:, lo:hi].bitcast(FP8X4), scales=ws[:, lo:hi], in_=src[:].rearrange("p t c j -> p (t c j)"))

        def product(t, lo, hi, copy, tag=None):
            bank = psum.tile([P, hi - lo], F32, name=f"bank{t}_{lo}", tag=tag or f"bank{t}_{lo}")
            nc.tensor.matmul_mx(
                out=bank[:],
                lhsT=wq[:, P * t : P * t + P].bitcast(FP8X4),
                lhsT_scale=ws[:, P * t : P * t + P],
                rhs=xw_g[:, lo:hi].bitcast(FP8X4),
                rhs_scale=xs_g[:, lo:hi],
                start=True,
                stop=True,
            )
            copy(y[t][:, lo:hi], bank[:])

        cast_w(nc.scalar.copy, 0, 0, 0, 2)
        cast_w(nc.scalar.copy, 0, 0, 2, 4)
        cast_w(nc.scalar.copy, 0, 1)
        quant_w(w_lo[0], 0, P)
        for lo, hi in ((0, 256), (256, 384), (384, 512)):
            nc.vector.tensor_copy(xw_g[:, lo:hi], xw[:].bitcast(U32).indirect(offs_t[:, lo // 16 : hi // 16]))
            product(0, lo, hi, nc.scalar.copy)
        nc.scalar.activation(omf[:], fr[:], mybir.ActivationFunctionType.Copy, bias=1.0, scale=-1.0)
        cast_w(nc.vector.tensor_copy, 1, 0)
        cast_w(nc.vector.tensor_copy, 1, 1)
        quant_w(w_lo[1], P, 2 * P)
        quant_w(w_hi, 2 * P, 4 * P)
        product(1, 0, 256, nc.scalar.copy)
        product(1, 256, 512, nc.scalar.copy)

        weighed = held.tile([P, 2, PACK * V], F32, name="weighed", tag="w_lo1", align_bytes=64)
        la = weighed[:, 0, :]
        rb = weighed[:, 1, :]
        ob = held.tile([P, V, PACK], BF16, name="ob", align_bytes=64)
        ow = held.tile([P, V], U32, name="ow", align_bytes=64)
        osc = held.tile([P, V], U8, name="osc", align_bytes=64)
        words_out = out_1[0].rearrange("p n r -> p (n r)").bitcast(I32)

        def g_left(t):
            nc.vector.tensor_tensor(la[:, t * V : t * V + V], y[t][:].indirect(left_t[:]), omf[:], MULT)

        def g_right(t):
            nc.vector.tensor_tensor(rb[:, t * V : t * V + V], y[t][:].indirect(right_t[:]), fr[:], MULT)

        lv = held.tile([P, 2 * V], F32, name="lv")

        def s_left(t, lo, hi):
            nc.scalar.activation(lv[:, (t - 2) * V + lo : (t - 2) * V + hi], y[t][:].indirect(left_t[:, lo // 16 : hi // 16]), mybir.ActivationFunctionType.Copy)

        def weigh(t, lo, hi):
            nc.vector.tensor_tensor(la[:, t * V + lo : t * V + hi], lv[:, (t - 2) * V + lo : (t - 2) * V + hi], omf[:, lo:hi], MULT)

        out_flat = out_0.rearrange("(p t) v -> p (t v)", t=PACK)

        def add(lo, hi):
            nc.vector.tensor_tensor(o[:, lo:hi], la[:, lo:hi], rb[:, lo:hi], ADD)

        turned = held.tile([P, 2, 2, P], F32, name="turned")

        def sum_turned(bank, i, h):
            cols = slice(V * i + P * h, V * i + P * h + P)
            nc.tensor.matmul(bank, rb[:, cols], ident[:], start=True, stop=False, is_transpose=True)
            nc.tensor.matmul(bank, la[:, cols], ident[:], start=False, stop=True, is_transpose=True)

        def turn_back(h):
            bank = psum.tile([P, 2, P], F32, name=f"bank_back{h}", tag=f"bank0_{256 * h}")
            for t in range(2):
                nc.tensor.transpose(bank[:, t, :], turned[:, h, t, :], ident[:])
            nc.scalar.copy(o[:].rearrange("p (t v) -> p t v", t=PACK)[:, 0:2, P * h : P * h + P], bank[:])

        def cast_o(copy, lo, hi):
            cols = slice(lo, hi)
            src = o[:].rearrange("p (t v) -> p t v", t=PACK)[:, :, cols]
            copy(ob[:, cols, :].rearrange("p (c i) t -> p c t i", i=2), src.rearrange("p t (c i) -> p c t i", i=2))

        def quant_o(h):
            cols = slice(128 * h, 128 * h + 128)
            nc.vector.quantize_mx(out=ow[:, cols].bitcast(FP8X4), scales=osc[:, cols], in_=ob[:, cols, :].rearrange("p v t -> p (v t)"))

        product(2, 0, 256, nc.scalar.copy)
        product(2, 256, 512, nc.scalar.copy, "bank0_0")
        product(3, 0, 256, nc.scalar.copy)
        product(3, 256, 512, nc.scalar.copy, "bank0_256")
        s_left(2, 0, V)
        g_right(0)
        g_left(0)
        sum0 = psum.tile([P, 2, P], F32, name="sum0", tag="sum0")
        for h in range(2):
            sum_turned(sum0[:, h, :], 0, h)
        nc.scalar.copy(turned[:, :, :, 0:64], sum0[:].rearrange("p h (c t) -> p h t c", t=2))
        s_left(3, P, V)
        g_right(1)
        sum1 = [psum.tile([P, P], F32, name=f"sum1{h}", tag=("bank0_384", "bank1_0")[h]) for h in range(2)]
        for h in (1, 0):
            nc.tensor.matmul(sum1[h][:], rb[:, V + P * h : V + P * h + P], ident[:], start=True, stop=False, is_transpose=True)
        g_left(1)
        for h in (1, 0):
            nc.tensor.matmul(sum1[h][:], la[:, V + P * h : V + P * h + P], ident[:], start=False, stop=True, is_transpose=True)
            nc.scalar.copy(turned[:, h, :, 64:P], sum1[h][:].rearrange("p (c t) -> p t c", t=2))
        s_left(3, 0, P)
        g_right(2)
        g_right(3)
        o = held.tile([P, PACK * V], F32, name="o", tag="y3")
        for h in (1, 0):
            turn_back(h)
        nc.sync.dma_start(out_flat[:, 0 : 2 * V], o[:, 0 : 2 * V])
        weigh(2, 0, V)
        weigh(3, P, V)
        weigh(3, 0, P)
        add(512, 768)
        nc.sync.dma_start(out_flat[:, 512:768], o[:, 512:768])
        add(896, 1024)
        add(768, 896)
        nc.sync.dma_start(out_flat[:, 768:1024], o[:, 768:1024])
        cast_o(nc.vector.tensor_copy, 128, 256)
        cast_o(nc.scalar.copy, 0, 80)
        cast_o(nc.vector.tensor_copy, 80, 128)
        quant_o(1)
        quant_o(0)
        nc.sync.dma_start(words_out, ow[:].bitcast(I32))
        for r in range(4):
            eng = nc.scalar if r % 2 == 0 else nc.sync
            eng.dma_start(out_2[0, r:16:4, :].bitcast(I32), osc[r:P:32, :].bitcast(I32))
